import numpy as np
CORES = [0,1,2,3,4,5,6,7]
N = 8
PERM = [[0,4],[1,5],[2,6],[3,7],[4,0],[5,1],[6,2],[7,3]]
def setup_inputs(rng):
    return {"x": rng.standard_normal((N, 128, 2048), dtype=np.float32)}
def reference(x):
    y = np.empty_like(x)
    for s, d in PERM:
        y[d] = x[s]
    return {"y": y}

@@ -1,0 +1,46 @@
+SCRATCH = {
+    "stage": ("sbuf", [128, 2048], "float32"),
+    "land": ("sbuf", [128, 2048], "float32"),
+}
+SEMAPHORES = ["loaded", "read", "arrived", "stored"]
+
+LOCAL_DONE = 16
+
+
+def rank_program(g, core, T, topo):
+    rank = T.rank_of(core)
+    if rank is None:
+        return
+
+    perm = T.tables["PERM"]
+    dsts = [d for s, d in perm if s == rank]
+    srcs = [s for s, d in perm if d == rank]
+
+    remote_dsts = [d for d in dsts if d != rank]
+    stored = 0
+
+    if rank in dsts:
+        g.dma_start(T.y[:], T.x[:]).then_inc(T.sem.stored, LOCAL_DONE)
+        stored += LOCAL_DONE
+
+    sent = 0
+    if remote_dsts:
+        g.dma_start(T.stage[:], T.x[:]).then_inc(T.sem.loaded, LOCAL_DONE)
+        g.wait_ge(T.sem.loaded, LOCAL_DONE)
+        for d in remote_dsts:
+            dst_core = T.cores[d]
+            rid, pid, _se = topo.addr(dst_core)
+            engines = topo.mask(core, dst_core)
+            g.remote_dma(T.land[:], T.stage[:], T.sem.arrived, T.sem.read, pid, rid, engines)
+            sent += bin(engines).count("1")
+
+    if srcs and srcs[0] != rank:
+        src_core = T.cores[srcs[0]]
+        g.wait_ge(T.sem.arrived, bin(topo.mask(src_core, core)).count("1"))
+        g.dma_start(T.y[:], T.land[:]).then_inc(T.sem.stored, LOCAL_DONE)
+        stored += LOCAL_DONE
+
+    if sent:
+        g.wait_ge(T.sem.read, sent)
+    if stored:
+        g.wait_ge(T.sem.stored, stored)

@@ -29,7 +29,8 @@ def rank_program(g, core, T, topo):
         g.wait_ge(T.sem.loaded, LOCAL_DONE)
         for d in remote_dsts:
             dst_core = T.cores[d]
-            rid, pid, _se = topo.addr(dst_core)
+            where = topo.addr(dst_core)
+            rid, pid = where[0], where[1]
             engines = topo.mask(core, dst_core)
             g.remote_dma(T.land[:], T.stage[:], T.sem.arrived, T.sem.read, pid, rid, engines)
             sent += bin(engines).count("1")

SCRATCH = {
    "stage": ("sbuf", [128, 2048], "float32"),
    "land": ("sbuf", [128, 2048], "float32"),
}
SEMAPHORES = ["loaded", "read", "arrived", "stored"]

LOCAL_DONE = 16


def rank_program(g, core, T, topo):
    rank = T.rank_of(core)
    if rank is None:
        return

    perm = T.tables["PERM"]
    dsts = [d for s, d in perm if s == rank]
    srcs = [s for s, d in perm if d == rank]

    remote_dsts = [d for d in dsts if d != rank]
    stored = 0

    if rank in dsts:
        g.dma_start(T.y[:], T.x[:]).then_inc(T.sem.stored, LOCAL_DONE)
        stored += LOCAL_DONE

    sent = 0
    if remote_dsts:
        g.dma_start(T.stage[:], T.x[:]).then_inc(T.sem.loaded, LOCAL_DONE)
        g.wait_ge(T.sem.loaded, LOCAL_DONE)
        for d in remote_dsts:
            dst_core = T.cores[d]
            where = topo.addr(dst_core)
            rid, pid = where[0], where[1]
            engines = topo.mask(core, dst_core)
            g.remote_dma(T.land[:], T.stage[:], T.sem.arrived, T.sem.read, pid, rid, engines)
            sent += bin(engines).count("1")

    if srcs and srcs[0] != rank:
        src_core = T.cores[srcs[0]]
        g.wait_ge(T.sem.arrived, bin(topo.mask(src_core, core)).count("1"))
        g.dma_start(T.y[:], T.land[:]).then_inc(T.sem.stored, LOCAL_DONE)
        stored += LOCAL_DONE

    if sent:
        g.wait_ge(T.sem.read, sent)
    if stored:
        g.wait_ge(T.sem.stored, stored)
